import numpy as np
import ml_dtypes


def mxq(x, axis, fmt="e4m3"):
    dtype, down = {"e4m3": (ml_dtypes.float8_e4m3fn, 7), "e5m2": (ml_dtypes.float8_e5m2, 14)}[fmt]
    v = np.moveaxis(np.asarray(x, np.float32).astype(ml_dtypes.bfloat16).astype(np.float64), axis, -1)
    blocks = v.reshape(v.shape[:-1] + (-1, 32))
    amax = np.abs(blocks).max(-1, keepdims=True)
    byte = np.maximum(np.where(amax > 0, np.frexp(amax)[1] - 1 + 127, 0) - down, 1)
    scale = np.exp2(byte - 127.0)
    codes = (blocks / scale).astype(np.float32).astype(dtype).astype(np.float64)
    return np.moveaxis((codes * scale).reshape(v.shape), -1, axis)


WIDE = False


def mx_kscale(k):
    if not WIDE:
        return np.ones(k)
    levels = np.array([10, -10, 5, -5, 0])
    if k % 512:
        return np.exp2(np.random.permutation(np.resize(levels, k // 32))).repeat(32)
    a = np.empty((k // 512, 16))
    for p in range(k // 512):
        a[p, :8] = np.random.permutation(np.resize(levels, 8))
        for g in range(8):
            far = levels[np.abs(levels - a[p, g]) >= 10]
            a[p, g + 8] = far[np.random.randint(len(far))]
    return np.exp2(a.ravel()).repeat(32)


def f64(x):
    return np.asarray(x).astype(np.float64)


def striped(idx):
    return np.tile(idx.reshape(-1, 16).T, (8, 1)).astype(np.uint16)


def unstriped(offs):
    return offs[:16].T.reshape(-1).astype(np.int64)


def striped8(idx):
    return np.concatenate([x.reshape(-1, 16).T for x in idx]).astype(np.uint16)


def runs(offs, k):
    lists = np.stack([offs[16 * r : 16 * r + 16].T.reshape(-1) for r in range(8)]).astype(np.int64)
    return lists[np.arange(k) % 512 // 64]


def pack_weight(w):
    k, n = w.shape
    w = f64(np.asarray(w, np.float32).astype(ml_dtypes.bfloat16)).reshape(k // 32, 32, n)
    amax = np.abs(w).max(1)
    byte = np.clip(np.where(amax > 0, np.frexp(amax)[1] - 1 + 127 - 7, 1), 1, 254)
    scaled = (w * np.exp2(127.0 - byte)[:, None, :]).reshape(k, n).astype(np.float32)
    words = np.ascontiguousarray(scaled.reshape(k // 512, 128, 4, n).transpose(0, 1, 3, 2)).astype(ml_dtypes.float8_e4m3fn).view(np.uint8)
    return words, np.ascontiguousarray(byte.astype(np.uint8).reshape(k // 512, 16, n))


def unpack_weight(words, scales):
    g, p, n, _ = words.shape
    vals = np.ascontiguousarray(words).view(ml_dtypes.float8_e4m3fn).astype(np.float64) * np.repeat(np.exp2(scales.astype(np.float64) - 127.0), 8, axis=1)[..., None]
    return vals.transpose(0, 1, 3, 2).reshape(g * 512, n)

def planes(y):
    n, m = y.shape
    v = y.astype(np.float32).astype(ml_dtypes.bfloat16).astype(np.float64).reshape(n // 32, 32, m)
    top = np.abs(v).max(1)
    byte = np.clip(np.where(top > 0, np.frexp(top)[1] - 1 + 127 - 7, 1), 1, 254)
    codes = (v * np.exp2(127.0 - byte)[:, None, :]).reshape(n, m).astype(np.float32).astype(ml_dtypes.float8_e4m3fn).view(np.uint8)
    words = codes.reshape(n // 512, 128, 4, m).transpose(0, 1, 3, 2)
    return np.ascontiguousarray(words), np.ascontiguousarray(byte.astype(np.uint8).reshape(n // 512, 16, m))


K, T, S, G, H, W = 512, 1024, 256, 2048, 512, 128


def setup_inputs():
    n = np.random.standard_normal
    s = mx_kscale(K)[:, None]
    packed_xT = pack_weight(n((K, T)) * s)
    packed_dT = pack_weight(n((K, G)) / s)
    perm = np.random.permutation(S)
    perm2 = np.random.permutation(S)
    perm3 = np.random.permutation(S)
    return {
        "x_words": packed_xT[0],
        "x_scales": packed_xT[1],
        "d_words": packed_dT[0],
        "d_scales": packed_dT[1],
        "gs": (np.random.uniform(0.5, 1.5, (K, 1)) * s).astype(np.float32),
        "offs": striped8(np.random.randint(0, T, (8, S))),
        "k1": striped8(np.random.randint(0, G, (8, H))),
        "hz": striped8(np.random.randint(0, T, (8, S))),
        "k2": striped8(np.random.randint(0, G, (8, H))),
        "n1": striped(perm[:W]),
        "n2": striped(perm[W:]),
        "n3": striped(np.random.permutation(S)),
        "k3": striped8(np.random.randint(0, G, (8, H))),
        "k4": striped8(np.random.randint(0, G, (8, H))),
        "two": striped(np.random.permutation(T)[:S]),
        "k5": striped8(np.random.randint(0, G, (8, H))),
        "hy": striped8(np.random.randint(0, T, (8, S))),
        "n4": striped(perm2[:W]),
        "n5": striped(perm2[W:]),
        "n6": striped(perm3[:W]),
        "n7": striped(perm3[W:]),
    }


def reference(x_words, x_scales, d_words, d_scales, gs, offs, k1, hz, k2, n1, n2, n3, k3, k4, two, k5, hy, n4, n5, n6, n7):
    d_k3 = unpack_weight(d_words, d_scales)[np.arange(K)[:, None], runs(k3, K)]
    d_k1 = unpack_weight(d_words, d_scales)[np.arange(K)[:, None], runs(k1, K)]
    xq = unpack_weight(x_words, x_scales)[np.arange(K)[:, None], runs(offs, K)]
    d_k2 = unpack_weight(d_words, d_scales)[np.arange(K)[:, None], runs(k2, K)]
    x_hz = unpack_weight(x_words, x_scales)[np.arange(K)[:, None], runs(hz, K)]
    h = 0.0625 * (d_k1.T @ xq + d_k2.T @ x_hz)
    pa = h[:, unstriped(n1)]
    pb = h[:, unstriped(n2)]
    rb = pa - pb
    ua = np.zeros((H, S))
    ua[:, unstriped(n1)] = pb
    ub = ua.copy()
    ub[:, unstriped(n2)] = rb
    z = f64(gs) * (np.maximum(ub, 0.5 * ub[:, unstriped(n3)]))
    d_k4 = unpack_weight(d_words, d_scales)[np.arange(K)[:, None], runs(k4, K)]
    x_two = unpack_weight(x_words, x_scales)[:, unstriped(two)]
    d_k5 = unpack_weight(d_words, d_scales)[np.arange(K)[:, None], runs(k5, K)]
    x_hy = unpack_weight(x_words, x_scales)[np.arange(K)[:, None], runs(hy, K)]
    h2 = 0.0625 * ((d_k3.T @ mxq(z, 0, "e4m3") + d_k4.T @ x_two + d_k5.T @ x_hy))
    pa2 = h2[:, unstriped(n4)]
    pb2 = h2[:, unstriped(n5)]
    rb2 = np.minimum(pa2, pb2)
    ra = np.maximum(pa2, pb2)
    ua2 = np.zeros((H, S))
    ua2[:, unstriped(n6)] = ra
    ub2 = ua2.copy()
    ub2[:, unstriped(n7)] = rb2
    out_0 = ub2 - h2
    return (out_0,) + planes(out_0)

@@ -1,0 +1,199 @@
+from contextlib import ExitStack
+
+import concourse.mybir as mybir
+
+F32 = mybir.dt.float32
+BF16 = mybir.dt.bfloat16
+I32 = mybir.dt.int32
+U32 = mybir.dt.uint32
+U16 = mybir.dt.uint16
+U8 = mybir.dt.uint8
+FP8X4 = mybir.dt.float8_e4m3fn_x4
+ALU = mybir.AluOpType
+COPY = mybir.ActivationFunctionType.Copy
+
+P = 128
+K, T, S, G, H, W = 512, 1024, 256, 2048, 512, 128
+PACK = 4
+FLOPS = 5 * 2 * K * H * S
+
+
+def tile_picked_mhhzmthswapdcpor_none_po_kernel(
+    tc, x_words, x_scales, d_words, d_scales, gs, offs, k1, hz, k2, n1, n2, n3, k3, k4, two, k5, hy, n4, n5, n6, n7,
+    out_0, out_1, out_2,
+):
+    nc = tc.nc
+    with ExitStack() as ctx:
+        held = ctx.enter_context(tc.tile_pool(name="held", bufs=1))
+        keep = ctx.enter_context(tc.tile_pool(name="keep", bufs=1))
+        psum = ctx.enter_context(tc.psum_pool(name="psum", bufs=1))
+
+        def load_list(name, source):
+            tile = held.tile([P, source.shape[1]], U16, name=name)
+            nc.sync.dma_start(tile[:], source)
+            return tile
+
+        def load_scale_window(name, source, width):
+            tile = keep.tile([P, width], U8, name=name, align_bytes=64)
+            nc.vector.memset(tile[:].bitcast(I32), 0)
+            nc.scalar.dma_start(out=tile[0:P:8, :].bitcast(I32), in_=source[0].bitcast(I32))
+            return tile
+
+        def load_word_window(name, source, width):
+            tile = keep.tile([P, width], U32, name=name, align_bytes=64)
+            nc.sync.dma_start(out=tile[:].bitcast(I32), in_=source[0].rearrange("p n t -> p (n t)").bitcast(I32))
+            return tile
+
+        xs_win = load_scale_window("xs_win", x_scales, T)
+        ds_win = load_scale_window("ds_win", d_scales, G)
+        L = {}
+        for name, source in (("offs", offs), ("hz", hz), ("k1", k1), ("k2", k2), ("n1", n1), ("n2", n2)):
+            L[name] = load_list(name, source)
+        dw_win = load_word_window("dw_win", d_words, G)
+        xw_win = load_word_window("xw_win", x_words, T)
+        for name, source in (("two", two), ("hy", hy), ("k4", k4), ("k5", k5), ("k3", k3),
+                             ("n3", n3), ("n4", n4), ("n5", n5), ("n6", n6), ("n7", n7)):
+            L[name] = load_list(name, source)
+        gs_sb = keep.tile([P, PACK], F32)
+        nc.gpsimd.dma_start(out=gs_sb[:], in_=gs.rearrange("(p t) o -> p (t o)", t=PACK))
+
+        def pick_bytes(picked, a0, names, window, width):
+            for a, name in enumerate(names):
+                nc.vector.tensor_copy(picked[:, a0 + a * width : a0 + (a + 1) * width], window[:].indirect(L[name][:]))
+
+        def place_planes(tag, picked, x_names, d_names):
+            nd = len(d_names)
+            width = nd * H + len(x_names) * S
+            planes = keep.tile([P, width], U8, name=tag + "_planes", align_bytes=64)
+            nc.vector.memset(planes[:].bitcast(I32), 0)
+            dealt = keep.tile([P, width], U8, name=tag + "_dealt", align_bytes=64)
+            nc.vector.tensor_copy(dealt[:, nd * H :].bitcast(I32), picked[:, nd * H : width].bitcast(I32))
+            nc.vector.tensor_copy(
+                dealt[:, : nd * H].rearrange("p (a t c i) -> p a c t i", a=nd, t=PACK, i=16),
+                picked[:, : nd * H].rearrange("p (a c i t) -> p a c t i", a=nd, t=PACK, i=16),
+            )
+            for q in range(4):
+                nc.sync.dma_start(
+                    out=planes[32 * q : 32 * q + 4, :].bitcast(I32), in_=dealt[32 * q : 32 * q + 32 : 8, :].bitcast(I32)
+                )
+            found = {name: planes[:, a * H : (a + 1) * H] for a, name in enumerate(d_names)}
+            for a, name in enumerate(x_names):
+                found[name] = planes[:, nd * H + a * S : nd * H + (a + 1) * S]
+            return found
+
+        def pick_words(name, window, width, tag):
+            picked = keep.tile([P, width], U32, name=name + "_words", tag=tag, align_bytes=64)
+            nc.vector.tensor_copy(picked[:], window[:].indirect(L[name][:]))
+            return picked
+
+        def deal_words(name, picked):
+            dealt = keep.tile([P, H], U32, name=name + "_dealt", align_bytes=64)
+            nc.vector.tensor_copy(
+                dealt[:].rearrange("p (t c i) -> p c t i", t=PACK, i=4),
+                picked[:].rearrange("p (c i t) -> p c t i", t=PACK, i=4),
+            )
+            return dealt
+
+        def product(acc, t, d_words_t, d_plane, codes, plane, start, stop):
+            cols = slice(t * P, (t + 1) * P)
+            nc.tensor.matmul_mx(
+                out=acc[:], lhsT=d_words_t[:, cols].bitcast(FP8X4), lhsT_scale=d_plane[:, cols],
+                rhs=codes.bitcast(FP8X4), rhs_scale=plane, start=start, stop=stop,
+            )
+
+        bytes1 = keep.tile([P, 2 * H + 2 * S], U8, align_bytes=64)
+        pick_bytes(bytes1, 2 * H, ("offs", "hz"), xs_win, S)
+        pick_bytes(bytes1, 0, ("k1", "k2"), ds_win, H)
+        planes1 = place_planes("first", bytes1, ("offs", "hz"), ("k1", "k2"))
+        w1 = pick_words("k1", dw_win, H, "slot_a")
+        w2 = pick_words("k2", dw_win, H, "slot_b")
+        d1 = deal_words("k1", w1)
+        xq = pick_words("offs", xw_win, S, "slot_c")
+        d2 = deal_words("k2", w2)
+        x_hz = pick_words("hz", xw_win, S, "slot_d")
+        acc1 = [psum.tile([P, S], F32, name="acc1_%d" % t) for t in range(PACK)]
+        for t in range(PACK):
+            product(acc1[t], t, d1, planes1["k1"], xq[:], planes1["offs"], True, False)
+        for t in range(PACK):
+            product(acc1[t], t, d2, planes1["k2"], x_hz[:], planes1["hz"], False, True)
+
+        bytes2 = keep.tile([P, 3 * H + 2 * S], U8, tag="slot_a", align_bytes=64)
+        pick_bytes(bytes2, 3 * H, ("two", "hy"), xs_win, S)
+        pick_bytes(bytes2, 0, ("k4", "k5", "k3"), ds_win, H)
+        planes2 = place_planes("second", bytes2, ("two", "hy"), ("k4", "k5", "k3"))
+        w4 = pick_words("k4", dw_win, H, "slot_b")
+        w5 = pick_words("k5", dw_win, H, "slot_a")
+        d4 = deal_words("k4", w4)
+        x_two = pick_words("two", xw_win, S, "slot_c")
+        d5 = deal_words("k5", w5)
+        w3 = pick_words("k3", dw_win, H, "slot_b")
+        x_hy = pick_words("hy", xw_win, S, "slot_d")
+        d3 = deal_words("k3", w3)
+        acc2 = [psum.tile([P, S], F32, name="acc2_%d" % t) for t in range(PACK)]
+        for t in range(PACK):
+            product(acc2[t], t, d4, planes2["k4"], x_two[:], planes2["two"], True, False)
+        for t in range(PACK):
+            product(acc2[t], t, d5, planes2["k5"], x_hy[:], planes2["hy"], False, False)
+
+        z_grouped = keep.tile([P, S, PACK], BF16, align_bytes=64)
+        for t in range(PACK):
+            h = keep.tile([P, S], F32, name="h_%d" % t)
+            nc.scalar.activation(h[:], acc1[t][:], COPY, scale=0.0625)
+            pa = keep.tile([P, W], F32, name="pa_%d" % t)
+            pb = keep.tile([P, W], F32, name="pb_%d" % t)
+            rb = keep.tile([P, W], F32, name="rb_%d" % t)
+            nc.scalar.activation(pa[:], h[:].indirect(L["n1"][:]), COPY)
+            nc.scalar.activation(pb[:], h[:].indirect(L["n2"][:]), COPY)
+            nc.gpsimd.tensor_tensor(rb[:], pa[:], pb[:], ALU.subtract)
+            ub = keep.tile([P, S], F32, name="ub_%d" % t)
+            nc.scalar.activation(ub[:].indirect(L["n1"][:]), pb[:], COPY)
+            nc.scalar.activation(ub[:].indirect(L["n2"][:]), rb[:], COPY)
+            far = keep.tile([P, S], F32, name="far_%d" % t)
+            for a in range(2):
+                nc.scalar.activation(far[:, a * W : (a + 1) * W], ub[:].indirect(L["n3"][:, 8 * a : 8 * (a + 1)]), COPY)
+            top = keep.tile([P, S], F32, name="top_%d" % t)
+            nc.vector.scalar_tensor_tensor(top[:], far[:], 0.5, ub[:], ALU.mult, ALU.max)
+            nc.vector.tensor_scalar(z_grouped[:, :, t], top[:], gs_sb[:, t : t + 1], None, ALU.mult)
+        z_codes = keep.tile([P, S], U32, align_bytes=64)
+        z_plane = keep.tile([P, S], U8, align_bytes=64)
+        nc.vector.quantize_mx(
+            out=z_codes[:].bitcast(FP8X4), scales=z_plane[:], in_=z_grouped[:].rearrange("p s t -> p (s t)")
+        )
+        for t in range(PACK):
+            product(acc2[t], t, d3, planes2["k3"], z_codes[:], z_plane[:], False, True)
+
+        y_grouped = keep.tile([P, S, PACK], BF16, align_bytes=64)
+        out_rows = out_0.rearrange("(p t) s -> p t s", t=PACK)
+        h2, high, low = [], [], []
+        for t in range(PACK):
+            h2.append(keep.tile([P, S], F32, name="h2_%d" % t))
+            if t == 0:
+                nc.scalar.activation(h2[t][:], acc2[t][:], COPY, scale=0.0625)
+            else:
+                nc.vector.tensor_scalar(h2[t][:], acc2[t][:], 0.0625, None, ALU.mult)
+        for t in range(PACK):
+            pa2 = keep.tile([P, W], F32, name="pa2_%d" % t)
+            pb2 = keep.tile([P, W], F32, name="pb2_%d" % t)
+            nc.scalar.activation(pa2[:], h2[t][:].indirect(L["n4"][:]), COPY)
+            nc.scalar.activation(pb2[:], h2[t][:].indirect(L["n5"][:]), COPY)
+            high.append(keep.tile([P, W], F32, name="high_%d" % t))
+            low.append(keep.tile([P, W], F32, name="low_%d" % t))
+            nc.vector.tensor_tensor(high[t][:], pa2[:], pb2[:], ALU.max)
+            nc.vector.tensor_tensor(low[t][:], pa2[:], pb2[:], ALU.min)
+        for t in range(PACK):
+            ub2 = keep.tile([P, S], F32, name="ub2_%d" % t)
+            nc.scalar.activation(ub2[:].indirect(L["n6"][:]), high[t][:], COPY)
+            nc.scalar.activation(ub2[:].indirect(L["n7"][:]), low[t][:], COPY)
+            y = keep.tile([P, S], F32, name="y_%d" % t)
+            nc.vector.tensor_tensor(y[:], ub2[:], h2[t][:], ALU.subtract)
+            nc.sync.dma_start(out=out_rows[:, t, :], in_=y[:])
+            nc.vector.tensor_copy(y_grouped[:, :, t], y[:])
+        y_codes = keep.tile([P, S], U32, align_bytes=64)
+        y_plane = keep.tile([P, S], U8, align_bytes=64)
+        nc.vector.quantize_mx(
+            out=y_codes[:].bitcast(FP8X4), scales=y_plane[:], in_=y_grouped[:].rearrange("p s t -> p (s t)")
+        )
+        nc.sync.dma_start(out=out_1[0].rearrange("p s t -> p (s t)").bitcast(I32), in_=y_codes[:].bitcast(I32))
+        for q in range(4):
+            queue = nc.scalar if q % 2 == 0 else nc.sync
+            queue.dma_start(out=out_2[0][4 * q : 4 * q + 4, :].bitcast(I32), in_=y_plane[32 * q : 32 * q + 4, :].bitcast(I32))

@@ -33,9 +33,9 @@ def tile_picked_mhhzmthswapdcpor_none_po_kernel(
             nc.sync.dma_start(tile[:], source)
             return tile
 
-        def load_scale_window(name, source, width):
+        def load_scale_window(name, source, width, engine):
             tile = keep.tile([P, width], U8, name=name, align_bytes=64)
-            nc.vector.memset(tile[:].bitcast(I32), 0)
+            engine.memset(tile[:].bitcast(I32), 0)
             nc.scalar.dma_start(out=tile[0:P:8, :].bitcast(I32), in_=source[0].bitcast(I32))
             return tile
 
@@ -44,155 +44,253 @@ def tile_picked_mhhzmthswapdcpor_none_po_kernel(
             nc.sync.dma_start(out=tile[:].bitcast(I32), in_=source[0].rearrange("p n t -> p (n t)").bitcast(I32))
             return tile
 
-        xs_win = load_scale_window("xs_win", x_scales, T)
-        ds_win = load_scale_window("ds_win", d_scales, G)
+        xs_win = load_scale_window("xs_win", x_scales, T, nc.gpsimd)
+        ds_win = load_scale_window("ds_win", d_scales, G, nc.vector)
         L = {}
         for name, source in (("offs", offs), ("hz", hz), ("k1", k1), ("k2", k2), ("n1", n1), ("n2", n2)):
             L[name] = load_list(name, source)
         dw_win = load_word_window("dw_win", d_words, G)
+        for name, source in (("two", two), ("hy", hy), ("k4", k4), ("k5", k5), ("k3", k3), ("n3", n3)):
+            L[name] = load_list(name, source)
         xw_win = load_word_window("xw_win", x_words, T)
-        for name, source in (("two", two), ("hy", hy), ("k4", k4), ("k5", k5), ("k3", k3),
-                             ("n3", n3), ("n4", n4), ("n5", n5), ("n6", n6), ("n7", n7)):
+        for name, source in (("n4", n4), ("n5", n5), ("n6", n6), ("n7", n7)):
             L[name] = load_list(name, source)
         gs_sb = keep.tile([P, PACK], F32)
         nc.gpsimd.dma_start(out=gs_sb[:], in_=gs.rearrange("(p t) o -> p (t o)", t=PACK))
 
-        def pick_bytes(picked, a0, names, window, width):
-            for a, name in enumerate(names):
-                nc.vector.tensor_copy(picked[:, a0 + a * width : a0 + (a + 1) * width], window[:].indirect(L[name][:]))
+        def pick_bytes(picked, first, name, window, width):
+            nc.vector.tensor_copy(picked[:, first : first + width], window[:].indirect(L[name][:]))
 
-        def place_planes(tag, picked, x_names, d_names):
-            nd = len(d_names)
-            width = nd * H + len(x_names) * S
-            planes = keep.tile([P, width], U8, name=tag + "_planes", align_bytes=64)
+        def blank_planes(name, width):
+            planes = keep.tile([P, width], U8, name=name, align_bytes=64)
             nc.vector.memset(planes[:].bitcast(I32), 0)
-            dealt = keep.tile([P, width], U8, name=tag + "_dealt", align_bytes=64)
-            nc.vector.tensor_copy(dealt[:, nd * H :].bitcast(I32), picked[:, nd * H : width].bitcast(I32))
-            nc.vector.tensor_copy(
-                dealt[:, : nd * H].rearrange("p (a t c i) -> p a c t i", a=nd, t=PACK, i=16),
-                picked[:, : nd * H].rearrange("p (a c i t) -> p a c t i", a=nd, t=PACK, i=16),
-            )
+            return planes
+
+        def move_rows(planes, level, picked, first, width):
             for q in range(4):
+                row = 32 * q + 4 * level
                 nc.sync.dma_start(
-                    out=planes[32 * q : 32 * q + 4, :].bitcast(I32), in_=dealt[32 * q : 32 * q + 32 : 8, :].bitcast(I32)
+                    out=planes[row : row + 4, :width].bitcast(I32),
+                    in_=picked[32 * q : 32 * q + 32 : 8, first : first + width].bitcast(I32),
                 )
-            found = {name: planes[:, a * H : (a + 1) * H] for a, name in enumerate(d_names)}
-            for a, name in enumerate(x_names):
-                found[name] = planes[:, nd * H + a * S : nd * H + (a + 1) * S]
-            return found
+
+        def deal(dealt, picked, run, t0, t1):
+            nc.vector.tensor_copy(
+                dealt.rearrange("p (t c i) -> p c t i", t=t1 - t0, i=run),
+                picked.rearrange("p (c i t) -> p c t i", t=PACK, i=run)[:, :, t0:t1, :],
+            )
 
         def pick_words(name, window, width, tag):
             picked = keep.tile([P, width], U32, name=name + "_words", tag=tag, align_bytes=64)
             nc.vector.tensor_copy(picked[:], window[:].indirect(L[name][:]))
             return picked
 
-        def deal_words(name, picked):
-            dealt = keep.tile([P, H], U32, name=name + "_dealt", align_bytes=64)
-            nc.vector.tensor_copy(
-                dealt[:].rearrange("p (t c i) -> p c t i", t=PACK, i=4),
-                picked[:].rearrange("p (c i t) -> p c t i", t=PACK, i=4),
-            )
-            return dealt
-
-        def product(acc, t, d_words_t, d_plane, codes, plane, start, stop):
-            cols = slice(t * P, (t + 1) * P)
+        def product(acc, d_codes, d_plane, codes, plane, start, stop):
             nc.tensor.matmul_mx(
-                out=acc[:], lhsT=d_words_t[:, cols].bitcast(FP8X4), lhsT_scale=d_plane[:, cols],
+                out=acc, lhsT=d_codes.bitcast(FP8X4), lhsT_scale=d_plane,
                 rhs=codes.bitcast(FP8X4), rhs_scale=plane, start=start, stop=stop,
             )
 
-        bytes1 = keep.tile([P, 2 * H + 2 * S], U8, align_bytes=64)
-        pick_bytes(bytes1, 2 * H, ("offs", "hz"), xs_win, S)
-        pick_bytes(bytes1, 0, ("k1", "k2"), ds_win, H)
-        planes1 = place_planes("first", bytes1, ("offs", "hz"), ("k1", "k2"))
+        def cols(t):
+            return slice(t * P, (t + 1) * P)
+
+        planes1 = blank_planes("planes1", 2 * H + 2 * S)
+        planes2 = blank_planes("planes2", H + S)
+        bytes_a = keep.tile([P, 2 * H + 2 * S], U8, tag="slot_e", align_bytes=64)
+        pick_bytes(bytes_a, 2 * H, "offs", xs_win, S)
+        pick_bytes(bytes_a, 2 * H + S, "hz", xs_win, S)
+        pick_bytes(bytes_a, 0, "k1", ds_win, H)
+        pick_bytes(bytes_a, H, "k2", ds_win, H)
+        move_rows(planes1, 0, bytes_a, 0, 2 * H + 2 * S)
         w1 = pick_words("k1", dw_win, H, "slot_a")
         w2 = pick_words("k2", dw_win, H, "slot_b")
-        d1 = deal_words("k1", w1)
+        d1_head = keep.tile([P, P], U32, tag="slot_g", align_bytes=64)
+        d2_head = keep.tile([P, P], U32, tag="slot_h", align_bytes=64)
+        deal(d1_head[:], w1[:], 4, 0, 1)
         xq = pick_words("offs", xw_win, S, "slot_c")
-        d2 = deal_words("k2", w2)
+        deal(d2_head[:], w2[:], 4, 0, 1)
         x_hz = pick_words("hz", xw_win, S, "slot_d")
+        dealt1 = keep.tile([P, PACK, 2 * P], U8, tag="slot_f", align_bytes=64)
+        deal(dealt1[:, 0, :], planes1[:, : 2 * H], 16, 0, 1)
+        deal(dealt1[:, 1:, :].rearrange("p t c -> p (t c)"), planes1[:, : 2 * H], 16, 1, PACK)
+        d_rest = keep.tile([P, 2, H - P], U32, tag="slot_e", align_bytes=64)
+        deal(d_rest[:, 0, :], w1[:], 4, 1, PACK)
+        deal(d_rest[:, 1, :], w2[:], 4, 1, PACK)
         acc1 = [psum.tile([P, S], F32, name="acc1_%d" % t) for t in range(PACK)]
         for t in range(PACK):
-            product(acc1[t], t, d1, planes1["k1"], xq[:], planes1["offs"], True, False)
-        for t in range(PACK):
-            product(acc1[t], t, d2, planes1["k2"], x_hz[:], planes1["hz"], False, True)
+            d1 = d1_head[:] if t == 0 else d_rest[:, 0, cols(t - 1)]
+            d2 = d2_head[:] if t == 0 else d_rest[:, 1, cols(t - 1)]
+            product(acc1[t][:], d1, dealt1[:, t, :P], xq[:], planes1[:, 2 * H : 2 * H + S], True, False)
+            product(acc1[t][:], d2, dealt1[:, t, P:], x_hz[:], planes1[:, 2 * H + S :], False, True)
 
-        bytes2 = keep.tile([P, 3 * H + 2 * S], U8, tag="slot_a", align_bytes=64)
-        pick_bytes(bytes2, 3 * H, ("two", "hy"), xs_win, S)
-        pick_bytes(bytes2, 0, ("k4", "k5", "k3"), ds_win, H)
-        planes2 = place_planes("second", bytes2, ("two", "hy"), ("k4", "k5", "k3"))
-        w4 = pick_words("k4", dw_win, H, "slot_b")
-        w5 = pick_words("k5", dw_win, H, "slot_a")
-        d4 = deal_words("k4", w4)
-        x_two = pick_words("two", xw_win, S, "slot_c")
-        d5 = deal_words("k5", w5)
-        w3 = pick_words("k3", dw_win, H, "slot_b")
-        x_hy = pick_words("hy", xw_win, S, "slot_d")
-        d3 = deal_words("k3", w3)
+        def tiles(name, width):
+            return [keep.tile([P, width], F32, name="%s_%d" % (name, t)) for t in range(PACK)]
+
+        h = tiles("h", S)
+        nc.scalar.activation(h[0][:], acc1[0][:], COPY, scale=0.0625)
+        x_two = pick_words("two", xw_win, S, "slot_g")
+        x_hy = pick_words("hy", xw_win, S, "slot_h")
+        for t in range(2, PACK):
+            nc.vector.tensor_scalar(h[t][:], acc1[t][:], 0.0625, None, ALU.mult)
+
+        bytes_c = keep.tile([P, H + S], U8, tag="slot_c", align_bytes=64)
+        bytes_d = keep.tile([P, 2 * H + S], U8, tag="slot_d", align_bytes=64)
+        pick_bytes(bytes_c, 0, "k4", ds_win, H)
+        pick_bytes(bytes_c, H, "two", xs_win, S)
+        move_rows(planes2, 0, bytes_c, 0, H + S)
+        pick_bytes(bytes_d, 0, "k5", ds_win, H)
+        pick_bytes(bytes_d, H, "hy", xs_win, S)
+        pick_bytes(bytes_d, H + S, "k3", ds_win, H)
+        move_rows(planes2, 1, bytes_d, 0, H + S)
+        move_rows(planes2, 2, bytes_d, H + S, H)
+        w4 = pick_words("k4", dw_win, H, "slot_e")
+        w5 = pick_words("k5", dw_win, H, "slot_f")
+        early = keep.tile([P, 3, 2 * P], U32, tag="slot_i", align_bytes=64)
+        deal(early[:, 0, :], w4[:], 4, 0, 2)
+        w3 = pick_words("k3", dw_win, H, "slot_c")
+        deal(early[:, 1, :], w5[:], 4, 0, 2)
+        early_planes = keep.tile([P, 2 * P], U8, tag="slot_j", align_bytes=64)
+        deal(early_planes[:], planes2[:, :H], 16, 0, 2)
+        deal(early[:, 2, :], w3[:], 4, 0, 2)
         acc2 = [psum.tile([P, S], F32, name="acc2_%d" % t) for t in range(PACK)]
-        for t in range(PACK):
-            product(acc2[t], t, d4, planes2["k4"], x_two[:], planes2["two"], True, False)
-        for t in range(PACK):
-            product(acc2[t], t, d5, planes2["k5"], x_hy[:], planes2["hy"], False, False)
+
+        def open_second(t, codes, planes):
+            part = cols(t % 2)
+            product(acc2[t][:], codes[:, 0, part], planes[:, part], x_two[:], planes2[:, H:], True, False)
+            product(acc2[t][:], codes[:, 1, part], planes[4:, part], x_hy[:], planes2[4:, H:], False, False)
+
+        for t in range(2):
+            open_second(t, early, early_planes)
 
         z_grouped = keep.tile([P, S, PACK], BF16, align_bytes=64)
-        for t in range(PACK):
-            h = keep.tile([P, S], F32, name="h_%d" % t)
-            nc.scalar.activation(h[:], acc1[t][:], COPY, scale=0.0625)
-            pa = keep.tile([P, W], F32, name="pa_%d" % t)
-            pb = keep.tile([P, W], F32, name="pb_%d" % t)
-            rb = keep.tile([P, W], F32, name="rb_%d" % t)
-            nc.scalar.activation(pa[:], h[:].indirect(L["n1"][:]), COPY)
-            nc.scalar.activation(pb[:], h[:].indirect(L["n2"][:]), COPY)
-            nc.gpsimd.tensor_tensor(rb[:], pa[:], pb[:], ALU.subtract)
-            ub = keep.tile([P, S], F32, name="ub_%d" % t)
-            nc.scalar.activation(ub[:].indirect(L["n1"][:]), pb[:], COPY)
-            nc.scalar.activation(ub[:].indirect(L["n2"][:]), rb[:], COPY)
-            far = keep.tile([P, S], F32, name="far_%d" % t)
-            for a in range(2):
-                nc.scalar.activation(far[:, a * W : (a + 1) * W], ub[:].indirect(L["n3"][:, 8 * a : 8 * (a + 1)]), COPY)
-            top = keep.tile([P, S], F32, name="top_%d" % t)
-            nc.vector.scalar_tensor_tensor(top[:], far[:], 0.5, ub[:], ALU.mult, ALU.max)
-            nc.vector.tensor_scalar(z_grouped[:, :, t], top[:], gs_sb[:, t : t + 1], None, ALU.mult)
         z_codes = keep.tile([P, S], U32, align_bytes=64)
         z_plane = keep.tile([P, S], U8, align_bytes=64)
-        nc.vector.quantize_mx(
-            out=z_codes[:].bitcast(FP8X4), scales=z_plane[:], in_=z_grouped[:].rearrange("p s t -> p (s t)")
-        )
+        ub, far = tiles("ub", S), tiles("far", S)
+        top = keep.tile([P, PACK, S], F32, tag="slot_d", align_bytes=64)
+        pa, pb, rb = tiles("pa", W), tiles("pb", W), tiles("rb", W)
+        halves = (slice(0, W), slice(W, S))
+
+        def fetch_pairs(t):
+            nc.scalar.activation(pb[t][:], h[t][:].indirect(L["n2"][:]), COPY)
+            nc.scalar.activation(pa[t][:], h[t][:].indirect(L["n1"][:]), COPY)
+            nc.gpsimd.tensor_tensor(rb[t][:], pa[t][:], pb[t][:], ALU.subtract)
+
+        def put_pb(t):
+            nc.scalar.activation(ub[t][:].indirect(L["n1"][:]), pb[t][:], COPY)
+
+        def put_rb(t):
+            nc.scalar.activation(ub[t][:].indirect(L["n2"][:]), rb[t][:], COPY)
+
+        def fetch_far(t, a):
+            nc.scalar.activation(far[t][:, halves[a]], ub[t][:].indirect(L["n3"][:, 8 * a : 8 * (a + 1)]), COPY)
+
+        def larger(t, part):
+            nc.vector.scalar_tensor_tensor(top[:, t, part], far[t][:, part], 0.5, ub[t][:, part], ALU.mult, ALU.max)
+
+        def weigh(t, part):
+            nc.vector.tensor_scalar(z_grouped[:, part, t], top[:, t, part], gs_sb[:, t : t + 1], None, ALU.mult)
+
         for t in range(PACK):
-            product(acc2[t], t, d3, planes2["k3"], z_codes[:], z_plane[:], False, True)
+            fetch_pairs(t)
+            if t == 0:
+                nc.scalar.activation(h[1][:], acc1[1][:], COPY, scale=0.0625)
+            if t >= 1:
+                put_rb(t - 1)
+            put_pb(t)
+            if t >= 1:
+                fetch_far(t - 1, 0)
+                if t == PACK - 1:
+                    put_rb(t)
+                fetch_far(t - 1, 1)
+        for a in range(2):
+            fetch_far(PACK - 1, a)
+        def quantise_z(part):
+            nc.vector.quantize_mx(
+                out=z_codes[:, part].bitcast(FP8X4), scales=z_plane[:, part],
+                in_=z_grouped[:, part, :].rearrange("p s t -> p (s t)"),
+            )
+
+        whole = slice(0, S)
+        left, right = halves
+        larger(0, whole)
+        larger(1, whole)
+        weigh(0, whole)
+        larger(2, left)
+        weigh(1, whole)
+        weigh(2, left)
+        larger(2, right)
+        larger(3, left)
+        weigh(2, right)
+        weigh(3, left)
+        larger(3, right)
+        quantise_z(left)
+        weigh(3, right)
+        quantise_z(right)
+        for a in range(2):
+            product(acc2[0][:, halves[a]], early[:, 2, cols(0)], early_planes[8:, cols(0)], z_codes[:, halves[a]],
+                    z_plane[:, halves[a]], False, a == 1)
+        product(acc2[1][:], early[:, 2, cols(1)], early_planes[8:, cols(1)], z_codes[:], z_plane[:], False, True)
+        h2 = tiles("h2", S)
+        nc.scalar.activation(h2[0][:], acc2[0][:], COPY, scale=0.0625)
+        nc.vector.tensor_scalar(h2[1][:], acc2[1][:], 0.0625, None, ALU.mult)
+        late = keep.tile([P, 3, 2 * P], U32, tag="slot_i", align_bytes=64)
+        late_planes = keep.tile([P, 2 * P], U8, tag="slot_j", align_bytes=64)
+        deal(late_planes[:], planes2[:, :H], 16, 2, PACK)
+        for a, picked in enumerate((w4, w5, w3)):
+            deal(late[:, a, :], picked[:], 4, 2, PACK)
+        for t in range(2, PACK):
+            open_second(t, late, late_planes)
+            product(acc2[t][:], late[:, 2, cols(t % 2)], late_planes[8:, cols(t % 2)], z_codes[:], z_plane[:], False, True)
+            nc.vector.tensor_scalar(h2[t][:], acc2[t][:], 0.0625, None, ALU.mult)
 
         y_grouped = keep.tile([P, S, PACK], BF16, align_bytes=64)
-        out_rows = out_0.rearrange("(p t) s -> p t s", t=PACK)
-        h2, high, low = [], [], []
-        for t in range(PACK):
-            h2.append(keep.tile([P, S], F32, name="h2_%d" % t))
-            if t == 0:
-                nc.scalar.activation(h2[t][:], acc2[t][:], COPY, scale=0.0625)
-            else:
-                nc.vector.tensor_scalar(h2[t][:], acc2[t][:], 0.0625, None, ALU.mult)
-        for t in range(PACK):
-            pa2 = keep.tile([P, W], F32, name="pa2_%d" % t)
-            pb2 = keep.tile([P, W], F32, name="pb2_%d" % t)
-            nc.scalar.activation(pa2[:], h2[t][:].indirect(L["n4"][:]), COPY)
-            nc.scalar.activation(pb2[:], h2[t][:].indirect(L["n5"][:]), COPY)
-            high.append(keep.tile([P, W], F32, name="high_%d" % t))
-            low.append(keep.tile([P, W], F32, name="low_%d" % t))
-            nc.vector.tensor_tensor(high[t][:], pa2[:], pb2[:], ALU.max)
-            nc.vector.tensor_tensor(low[t][:], pa2[:], pb2[:], ALU.min)
-        for t in range(PACK):
-            ub2 = keep.tile([P, S], F32, name="ub2_%d" % t)
-            nc.scalar.activation(ub2[:].indirect(L["n6"][:]), high[t][:], COPY)
-            nc.scalar.activation(ub2[:].indirect(L["n7"][:]), low[t][:], COPY)
-            y = keep.tile([P, S], F32, name="y_%d" % t)
-            nc.vector.tensor_tensor(y[:], ub2[:], h2[t][:], ALU.subtract)
-            nc.sync.dma_start(out=out_rows[:, t, :], in_=y[:])
-            nc.vector.tensor_copy(y_grouped[:, :, t], y[:])
         y_codes = keep.tile([P, S], U32, align_bytes=64)
         y_plane = keep.tile([P, S], U8, align_bytes=64)
-        nc.vector.quantize_mx(
-            out=y_codes[:].bitcast(FP8X4), scales=y_plane[:], in_=y_grouped[:].rearrange("p s t -> p (s t)")
-        )
+        out_rows = out_0.rearrange("(p t) s -> p t s", t=PACK)
+        ub2 = tiles("ub2", S)
+        y = keep.tile([P, PACK, S], F32)
+        pa2, pb2, high, low = tiles("pa2", W), tiles("pb2", W), tiles("high", W), tiles("low", W)
+
+        def fetch_a(t):
+            nc.scalar.activation(pa2[t][:], h2[t][:].indirect(L["n4"][:]), COPY)
+
+        def fetch_b(t):
+            nc.scalar.activation(pb2[t][:], h2[t][:].indirect(L["n5"][:]), COPY)
+            nc.vector.tensor_tensor(high[t][:], pa2[t][:], pb2[t][:], ALU.max)
+            nc.vector.tensor_tensor(low[t][:], pa2[t][:], pb2[t][:], ALU.min)
+
+        def put_high(t):
+            nc.scalar.activation(ub2[t][:].indirect(L["n6"][:]), high[t][:], COPY)
+
+        def put_low(t):
+            nc.scalar.activation(ub2[t][:].indirect(L["n7"][:]), low[t][:], COPY)
+            parts = halves if t == PACK - 1 else (slice(0, S),)
+            for part in parts:
+                nc.vector.tensor_tensor(y[:, t, part], ub2[t][:, part], h2[t][:, part], ALU.subtract)
+            nc.sync.dma_start(out=out_rows[:, t, :], in_=y[:, t, :])
+            if t % 2 == 1:
+                for part in parts:
+                    nc.vector.tensor_copy(
+                        y_grouped[:, part, t - 1 : t + 1], y[:, t - 1 : t + 1, part].rearrange("p t s -> p s t")
+                    )
+
+        for t in range(2):
+            fetch_a(t)
+            fetch_b(t)
+        for t in range(2):
+            put_high(t)
+            fetch_a(t + 2)
+            put_low(t)
+            fetch_b(t + 2)
+        put_high(2)
+        put_high(3)
+        put_low(2)
+        put_low(3)
+        for part in halves:
+            nc.vector.quantize_mx(
+                out=y_codes[:, part].bitcast(FP8X4), scales=y_plane[:, part],
+                in_=y_grouped[:, part, :].rearrange("p s t -> p (s t)"),
+            )
         nc.sync.dma_start(out=out_1[0].rearrange("p s t -> p (s t)").bitcast(I32), in_=y_codes[:].bitcast(I32))
         for q in range(4):
             queue = nc.scalar if q % 2 == 0 else nc.sync

from contextlib import ExitStack

import concourse.mybir as mybir

F32 = mybir.dt.float32
BF16 = mybir.dt.bfloat16
I32 = mybir.dt.int32
U32 = mybir.dt.uint32
U16 = mybir.dt.uint16
U8 = mybir.dt.uint8
FP8X4 = mybir.dt.float8_e4m3fn_x4
ALU = mybir.AluOpType
COPY = mybir.ActivationFunctionType.Copy

P = 128
K, T, S, G, H, W = 512, 1024, 256, 2048, 512, 128
PACK = 4
FLOPS = 5 * 2 * K * H * S


def tile_picked_mhhzmthswapdcpor_none_po_kernel(
    tc, x_words, x_scales, d_words, d_scales, gs, offs, k1, hz, k2, n1, n2, n3, k3, k4, two, k5, hy, n4, n5, n6, n7,
    out_0, out_1, out_2,
):
    nc = tc.nc
    with ExitStack() as ctx:
        held = ctx.enter_context(tc.tile_pool(name="held", bufs=1))
        keep = ctx.enter_context(tc.tile_pool(name="keep", bufs=1))
        psum = ctx.enter_context(tc.psum_pool(name="psum", bufs=1))

        def load_list(name, source):
            tile = held.tile([P, source.shape[1]], U16, name=name)
            nc.sync.dma_start(tile[:], source)
            return tile

        def load_scale_window(name, source, width, engine):
            tile = keep.tile([P, width], U8, name=name, align_bytes=64)
            engine.memset(tile[:].bitcast(I32), 0)
            nc.scalar.dma_start(out=tile[0:P:8, :].bitcast(I32), in_=source[0].bitcast(I32))
            return tile

        def load_word_window(name, source, width):
            tile = keep.tile([P, width], U32, name=name, align_bytes=64)
            nc.sync.dma_start(out=tile[:].bitcast(I32), in_=source[0].rearrange("p n t -> p (n t)").bitcast(I32))
            return tile

        xs_win = load_scale_window("xs_win", x_scales, T, nc.gpsimd)
        ds_win = load_scale_window("ds_win", d_scales, G, nc.vector)
        L = {}
        for name, source in (("offs", offs), ("hz", hz), ("k1", k1), ("k2", k2), ("n1", n1), ("n2", n2)):
            L[name] = load_list(name, source)
        dw_win = load_word_window("dw_win", d_words, G)
        for name, source in (("two", two), ("hy", hy), ("k4", k4), ("k5", k5), ("k3", k3), ("n3", n3)):
            L[name] = load_list(name, source)
        xw_win = load_word_window("xw_win", x_words, T)
        for name, source in (("n4", n4), ("n5", n5), ("n6", n6), ("n7", n7)):
            L[name] = load_list(name, source)
        gs_sb = keep.tile([P, PACK], F32)
        nc.gpsimd.dma_start(out=gs_sb[:], in_=gs.rearrange("(p t) o -> p (t o)", t=PACK))

        def pick_bytes(picked, first, name, window, width):
            nc.vector.tensor_copy(picked[:, first : first + width], window[:].indirect(L[name][:]))

        def blank_planes(name, width):
            planes = keep.tile([P, width], U8, name=name, align_bytes=64)
            nc.vector.memset(planes[:].bitcast(I32), 0)
            return planes

        def move_rows(planes, level, picked, first, width):
            for q in range(4):
                row = 32 * q + 4 * level
                nc.sync.dma_start(
                    out=planes[row : row + 4, :width].bitcast(I32),
                    in_=picked[32 * q : 32 * q + 32 : 8, first : first + width].bitcast(I32),
                )

        def deal(dealt, picked, run, t0, t1):
            nc.vector.tensor_copy(
                dealt.rearrange("p (t c i) -> p c t i", t=t1 - t0, i=run),
                picked.rearrange("p (c i t) -> p c t i", t=PACK, i=run)[:, :, t0:t1, :],
            )

        def pick_words(name, window, width, tag):
            picked = keep.tile([P, width], U32, name=name + "_words", tag=tag, align_bytes=64)
            nc.vector.tensor_copy(picked[:], window[:].indirect(L[name][:]))
            return picked

        def product(acc, d_codes, d_plane, codes, plane, start, stop):
            nc.tensor.matmul_mx(
                out=acc, lhsT=d_codes.bitcast(FP8X4), lhsT_scale=d_plane,
                rhs=codes.bitcast(FP8X4), rhs_scale=plane, start=start, stop=stop,
            )

        def cols(t):
            return slice(t * P, (t + 1) * P)

        planes1 = blank_planes("planes1", 2 * H + 2 * S)
        planes2 = blank_planes("planes2", H + S)
        bytes_a = keep.tile([P, 2 * H + 2 * S], U8, tag="slot_e", align_bytes=64)
        pick_bytes(bytes_a, 2 * H, "offs", xs_win, S)
        pick_bytes(bytes_a, 2 * H + S, "hz", xs_win, S)
        pick_bytes(bytes_a, 0, "k1", ds_win, H)
        pick_bytes(bytes_a, H, "k2", ds_win, H)
        move_rows(planes1, 0, bytes_a, 0, 2 * H + 2 * S)
        w1 = pick_words("k1", dw_win, H, "slot_a")
        w2 = pick_words("k2", dw_win, H, "slot_b")
        d1_head = keep.tile([P, P], U32, tag="slot_g", align_bytes=64)
        d2_head = keep.tile([P, P], U32, tag="slot_h", align_bytes=64)
        deal(d1_head[:], w1[:], 4, 0, 1)
        xq = pick_words("offs", xw_win, S, "slot_c")
        deal(d2_head[:], w2[:], 4, 0, 1)
        x_hz = pick_words("hz", xw_win, S, "slot_d")
        dealt1 = keep.tile([P, PACK, 2 * P], U8, tag="slot_f", align_bytes=64)
        deal(dealt1[:, 0, :], planes1[:, : 2 * H], 16, 0, 1)
        deal(dealt1[:, 1:, :].rearrange("p t c -> p (t c)"), planes1[:, : 2 * H], 16, 1, PACK)
        d_rest = keep.tile([P, 2, H - P], U32, tag="slot_e", align_bytes=64)
        deal(d_rest[:, 0, :], w1[:], 4, 1, PACK)
        deal(d_rest[:, 1, :], w2[:], 4, 1, PACK)
        acc1 = [psum.tile([P, S], F32, name="acc1_%d" % t) for t in range(PACK)]
        for t in range(PACK):
            d1 = d1_head[:] if t == 0 else d_rest[:, 0, cols(t - 1)]
            d2 = d2_head[:] if t == 0 else d_rest[:, 1, cols(t - 1)]
            product(acc1[t][:], d1, dealt1[:, t, :P], xq[:], planes1[:, 2 * H : 2 * H + S], True, False)
            product(acc1[t][:], d2, dealt1[:, t, P:], x_hz[:], planes1[:, 2 * H + S :], False, True)

        def tiles(name, width):
            return [keep.tile([P, width], F32, name="%s_%d" % (name, t)) for t in range(PACK)]

        h = tiles("h", S)
        nc.scalar.activation(h[0][:], acc1[0][:], COPY, scale=0.0625)
        x_two = pick_words("two", xw_win, S, "slot_g")
        x_hy = pick_words("hy", xw_win, S, "slot_h")
        for t in range(2, PACK):
            nc.vector.tensor_scalar(h[t][:], acc1[t][:], 0.0625, None, ALU.mult)

        bytes_c = keep.tile([P, H + S], U8, tag="slot_c", align_bytes=64)
        bytes_d = keep.tile([P, 2 * H + S], U8, tag="slot_d", align_bytes=64)
        pick_bytes(bytes_c, 0, "k4", ds_win, H)
        pick_bytes(bytes_c, H, "two", xs_win, S)
        move_rows(planes2, 0, bytes_c, 0, H + S)
        pick_bytes(bytes_d, 0, "k5", ds_win, H)
        pick_bytes(bytes_d, H, "hy", xs_win, S)
        pick_bytes(bytes_d, H + S, "k3", ds_win, H)
        move_rows(planes2, 1, bytes_d, 0, H + S)
        move_rows(planes2, 2, bytes_d, H + S, H)
        w4 = pick_words("k4", dw_win, H, "slot_e")
        w5 = pick_words("k5", dw_win, H, "slot_f")
        early = keep.tile([P, 3, 2 * P], U32, tag="slot_i", align_bytes=64)
        deal(early[:, 0, :], w4[:], 4, 0, 2)
        w3 = pick_words("k3", dw_win, H, "slot_c")
        deal(early[:, 1, :], w5[:], 4, 0, 2)
        early_planes = keep.tile([P, 2 * P], U8, tag="slot_j", align_bytes=64)
        deal(early_planes[:], planes2[:, :H], 16, 0, 2)
        deal(early[:, 2, :], w3[:], 4, 0, 2)
        acc2 = [psum.tile([P, S], F32, name="acc2_%d" % t) for t in range(PACK)]

        def open_second(t, codes, planes):
            part = cols(t % 2)
            product(acc2[t][:], codes[:, 0, part], planes[:, part], x_two[:], planes2[:, H:], True, False)
            product(acc2[t][:], codes[:, 1, part], planes[4:, part], x_hy[:], planes2[4:, H:], False, False)

        for t in range(2):
            open_second(t, early, early_planes)

        z_grouped = keep.tile([P, S, PACK], BF16, align_bytes=64)
        z_codes = keep.tile([P, S], U32, align_bytes=64)
        z_plane = keep.tile([P, S], U8, align_bytes=64)
        ub, far = tiles("ub", S), tiles("far", S)
        top = keep.tile([P, PACK, S], F32, tag="slot_d", align_bytes=64)
        pa, pb, rb = tiles("pa", W), tiles("pb", W), tiles("rb", W)
        halves = (slice(0, W), slice(W, S))

        def fetch_pairs(t):
            nc.scalar.activation(pb[t][:], h[t][:].indirect(L["n2"][:]), COPY)
            nc.scalar.activation(pa[t][:], h[t][:].indirect(L["n1"][:]), COPY)
            nc.gpsimd.tensor_tensor(rb[t][:], pa[t][:], pb[t][:], ALU.subtract)

        def put_pb(t):
            nc.scalar.activation(ub[t][:].indirect(L["n1"][:]), pb[t][:], COPY)

        def put_rb(t):
            nc.scalar.activation(ub[t][:].indirect(L["n2"][:]), rb[t][:], COPY)

        def fetch_far(t, a):
            nc.scalar.activation(far[t][:, halves[a]], ub[t][:].indirect(L["n3"][:, 8 * a : 8 * (a + 1)]), COPY)

        def larger(t, part):
            nc.vector.scalar_tensor_tensor(top[:, t, part], far[t][:, part], 0.5, ub[t][:, part], ALU.mult, ALU.max)

        def weigh(t, part):
            nc.vector.tensor_scalar(z_grouped[:, part, t], top[:, t, part], gs_sb[:, t : t + 1], None, ALU.mult)

        for t in range(PACK):
            fetch_pairs(t)
            if t == 0:
                nc.scalar.activation(h[1][:], acc1[1][:], COPY, scale=0.0625)
            if t >= 1:
                put_rb(t - 1)
            put_pb(t)
            if t >= 1:
                fetch_far(t - 1, 0)
                if t == PACK - 1:
                    put_rb(t)
                fetch_far(t - 1, 1)
        for a in range(2):
            fetch_far(PACK - 1, a)
        def quantise_z(part):
            nc.vector.quantize_mx(
                out=z_codes[:, part].bitcast(FP8X4), scales=z_plane[:, part],
                in_=z_grouped[:, part, :].rearrange("p s t -> p (s t)"),
            )

        whole = slice(0, S)
        left, right = halves
        larger(0, whole)
        larger(1, whole)
        weigh(0, whole)
        larger(2, left)
        weigh(1, whole)
        weigh(2, left)
        larger(2, right)
        larger(3, left)
        weigh(2, right)
        weigh(3, left)
        larger(3, right)
        quantise_z(left)
        weigh(3, right)
        quantise_z(right)
        for a in range(2):
            product(acc2[0][:, halves[a]], early[:, 2, cols(0)], early_planes[8:, cols(0)], z_codes[:, halves[a]],
                    z_plane[:, halves[a]], False, a == 1)
        product(acc2[1][:], early[:, 2, cols(1)], early_planes[8:, cols(1)], z_codes[:], z_plane[:], False, True)
        h2 = tiles("h2", S)
        nc.scalar.activation(h2[0][:], acc2[0][:], COPY, scale=0.0625)
        nc.vector.tensor_scalar(h2[1][:], acc2[1][:], 0.0625, None, ALU.mult)
        late = keep.tile([P, 3, 2 * P], U32, tag="slot_i", align_bytes=64)
        late_planes = keep.tile([P, 2 * P], U8, tag="slot_j", align_bytes=64)
        deal(late_planes[:], planes2[:, :H], 16, 2, PACK)
        for a, picked in enumerate((w4, w5, w3)):
            deal(late[:, a, :], picked[:], 4, 2, PACK)
        for t in range(2, PACK):
            open_second(t, late, late_planes)
            product(acc2[t][:], late[:, 2, cols(t % 2)], late_planes[8:, cols(t % 2)], z_codes[:], z_plane[:], False, True)
            nc.vector.tensor_scalar(h2[t][:], acc2[t][:], 0.0625, None, ALU.mult)

        y_grouped = keep.tile([P, S, PACK], BF16, align_bytes=64)
        y_codes = keep.tile([P, S], U32, align_bytes=64)
        y_plane = keep.tile([P, S], U8, align_bytes=64)
        out_rows = out_0.rearrange("(p t) s -> p t s", t=PACK)
        ub2 = tiles("ub2", S)
        y = keep.tile([P, PACK, S], F32)
        pa2, pb2, high, low = tiles("pa2", W), tiles("pb2", W), tiles("high", W), tiles("low", W)

        def fetch_a(t):
            nc.scalar.activation(pa2[t][:], h2[t][:].indirect(L["n4"][:]), COPY)

        def fetch_b(t):
            nc.scalar.activation(pb2[t][:], h2[t][:].indirect(L["n5"][:]), COPY)
            nc.vector.tensor_tensor(high[t][:], pa2[t][:], pb2[t][:], ALU.max)
            nc.vector.tensor_tensor(low[t][:], pa2[t][:], pb2[t][:], ALU.min)

        def put_high(t):
            nc.scalar.activation(ub2[t][:].indirect(L["n6"][:]), high[t][:], COPY)

        def put_low(t):
            nc.scalar.activation(ub2[t][:].indirect(L["n7"][:]), low[t][:], COPY)
            parts = halves if t == PACK - 1 else (slice(0, S),)
            for part in parts:
                nc.vector.tensor_tensor(y[:, t, part], ub2[t][:, part], h2[t][:, part], ALU.subtract)
            nc.sync.dma_start(out=out_rows[:, t, :], in_=y[:, t, :])
            if t % 2 == 1:
                for part in parts:
                    nc.vector.tensor_copy(
                        y_grouped[:, part, t - 1 : t + 1], y[:, t - 1 : t + 1, part].rearrange("p t s -> p s t")
                    )

        for t in range(2):
            fetch_a(t)
            fetch_b(t)
        for t in range(2):
            put_high(t)
            fetch_a(t + 2)
            put_low(t)
            fetch_b(t + 2)
        put_high(2)
        put_high(3)
        put_low(2)
        put_low(3)
        for part in halves:
            nc.vector.quantize_mx(
                out=y_codes[:, part].bitcast(FP8X4), scales=y_plane[:, part],
                in_=y_grouped[:, part, :].rearrange("p s t -> p (s t)"),
            )
        nc.sync.dma_start(out=out_1[0].rearrange("p s t -> p (s t)").bitcast(I32), in_=y_codes[:].bitcast(I32))
        for q in range(4):
            queue = nc.scalar if q % 2 == 0 else nc.sync
            queue.dma_start(out=out_2[0][4 * q : 4 * q + 4, :].bitcast(I32), in_=y_plane[32 * q : 32 * q + 4, :].bitcast(I32))
